import numpy as np
import ml_dtypes


def mxq(x, axis, fmt="e4m3"):
    dtype, down = {"e4m3": (ml_dtypes.float8_e4m3fn, 7), "e5m2": (ml_dtypes.float8_e5m2, 14)}[fmt]
    v = np.moveaxis(np.asarray(x, np.float32).astype(ml_dtypes.bfloat16).astype(np.float64), axis, -1)
    blocks = v.reshape(v.shape[:-1] + (-1, 32))
    amax = np.abs(blocks).max(-1, keepdims=True)
    byte = np.maximum(np.where(amax > 0, np.frexp(amax)[1] - 1 + 127, 0) - down, 1)
    scale = np.exp2(byte - 127.0)
    codes = (blocks / scale).astype(np.float32).astype(dtype).astype(np.float64)
    return np.moveaxis((codes * scale).reshape(v.shape), -1, axis)


WIDE = False


def mx_kscale(k):
    if not WIDE:
        return np.ones(k)
    levels = np.array([10, -10, 5, -5, 0])
    if k % 512:
        return np.exp2(np.random.permutation(np.resize(levels, k // 32))).repeat(32)
    a = np.empty((k // 512, 16))
    for p in range(k // 512):
        a[p, :8] = np.random.permutation(np.resize(levels, 8))
        for g in range(8):
            far = levels[np.abs(levels - a[p, g]) >= 10]
            a[p, g + 8] = far[np.random.randint(len(far))]
    return np.exp2(a.ravel()).repeat(32)


def f64(x):
    return np.asarray(x).astype(np.float64)


def striped(idx):
    return np.tile(idx.reshape(-1, 16).T, (8, 1)).astype(np.uint16)


def unstriped(offs):
    return offs[:16].T.reshape(-1).astype(np.int64)


def relu(v):
    return np.maximum(v, 0.0)

def planes(y):
    n, m = y.shape
    v = y.astype(np.float32).astype(ml_dtypes.bfloat16).astype(np.float64).reshape(n // 32, 32, m)
    top = np.abs(v).max(1)
    byte = np.clip(np.where(top > 0, np.frexp(top)[1] - 1 + 127 - 7, 1), 1, 254)
    codes = (v * np.exp2(127.0 - byte)[:, None, :]).reshape(n, m).astype(np.float32).astype(ml_dtypes.float8_e4m3fn).view(np.uint8)
    words = codes.reshape(n // 512, 128, 4, m).transpose(0, 1, 3, 2)
    return np.ascontiguousarray(words), np.ascontiguousarray(byte.astype(np.uint8).reshape(n // 512, 16, m))


K, T, S, V, N = 512, 1024, 512, 256, 512


def setup_inputs():
    n = np.random.standard_normal
    s = mx_kscale(K)[:, None]
    return {
        "xT": (n((K, T)) * s).astype(np.float32),
        "w1": (n((K, N)) / np.sqrt(K) / s).astype(np.float32),
        "w2": (n((K, N)) / np.sqrt(K) / s).astype(np.float32),
        "w3": (n((K, N)) / np.sqrt(K) / s).astype(np.float32),
        "offs": striped(np.random.permutation(T)[:S]),
        "cen": striped(np.random.permutation(S)[:V]),
        "pos1": striped(np.random.permutation(S)[:V]),
        "pos2": striped(np.random.permutation(S)[:V]),
    }


def reference(xT, w1, w2, w3, offs, cen, pos1, pos2):
    xq = mxq(f64(xT)[:, unstriped(offs)], 0, "e4m3")
    h = mxq(f64(w3), 0, "e4m3").T @ xq
    g = mxq(f64(w1), 0, "e4m3").T @ xq
    gc = g[:, unstriped(cen)]
    s = mxq(f64(w2), 0, "e4m3").T @ xq
    sc = s[:, unstriped(cen)]
    out_0 = relu(h[:, unstriped(pos1)] * gc + sc) + relu(h[:, unstriped(pos2)] * gc + sc)
    return (out_0,) + planes(out_0)

@@ -1,0 +1,163 @@
+from contextlib import ExitStack
+
+import concourse.mybir as mybir
+
+K, T, S, V, N = 512, 1024, 512, 256, 512
+FLOPS = 3 * 2 * K * N * S
+
+F32 = mybir.dt.float32
+BF16 = mybir.dt.bfloat16
+I32 = mybir.dt.int32
+U32 = mybir.dt.uint32
+U16 = mybir.dt.uint16
+U8 = mybir.dt.uint8
+FP8X4 = mybir.dt.float8_e4m3fn_x4
+MULT = mybir.AluOpType.mult
+ADD = mybir.AluOpType.add
+MAX = mybir.AluOpType.max
+RELU = mybir.ActivationFunctionType.Relu
+
+P = 128
+PACK = 4
+
+
+def tile_picked_filmg_relu_lo_kernel(
+    tc, xT, w1, w2, w3, offs, cen, pos1, pos2, out_0, out_1, out_2
+):
+    nc = tc.nc
+    with ExitStack() as ctx:
+        keep = ctx.enter_context(tc.tile_pool(name="keep", bufs=1))
+        psum = ctx.enter_context(tc.psum_pool(name="psum", bufs=8))
+
+        def load_list(src, name):
+            tile = keep.tile([P, src.shape[1]], U16, name=name)
+            nc.sync.dma_start(tile[:], src)
+            return tile
+
+        def load_weight(w, pieces, name):
+            width = N // pieces
+            rows = w.rearrange("(p j) c -> p j c", j=PACK)
+            raws = []
+            for i in range(pieces):
+                raw = keep.tile([P, PACK, width], F32, name="%s_raw%d" % (name, i))
+                nc.sync.dma_start(raw[:], rows[:, :, i * width : (i + 1) * width])
+                raws.append(raw)
+            return raws
+
+        def deal_weight(raws, copies, name):
+            dealt = keep.tile([P, PACK, P, PACK], BF16, name=name + "_dealt", align_bytes=64)
+            ms = P // len(raws)
+            for i, raw in enumerate(raws):
+                copies[i](
+                    dealt[:, :, i * ms : (i + 1) * ms, :].rearrange("p t m j -> p m j t"),
+                    raw[:].rearrange("p j (m t) -> p m j t", t=PACK),
+                )
+            return dealt
+
+        def quantize(src, cols, name, calls=1):
+            codes = keep.tile([P, cols], U32, name=name + "_codes", align_bytes=64)
+            scales = keep.tile([P, cols], U8, name=name + "_scales", align_bytes=64)
+            step = cols // calls
+            for i in range(calls):
+                nc.vector.quantize_mx(
+                    out=codes[:, i * step : (i + 1) * step].bitcast(FP8X4),
+                    scales=scales[:, i * step : (i + 1) * step],
+                    in_=src[:, i * step * PACK : (i + 1) * step * PACK],
+                )
+            return codes, scales
+
+        def product(wq, xq, name):
+            rows = []
+            for t in range(PACK):
+                acc = psum.tile([P, S], F32, name="acc")
+                cols = slice(t * P, (t + 1) * P)
+                nc.tensor.matmul_mx(
+                    out=acc[:],
+                    lhsT=wq[0][:, cols].bitcast(FP8X4),
+                    lhsT_scale=wq[1][:, cols],
+                    rhs=xq[0][:].bitcast(FP8X4),
+                    rhs_scale=xq[1][:],
+                    start=True,
+                    stop=True,
+                )
+                res = keep.tile([P, S], F32, name="%s%d" % (name, t))
+                nc.scalar.copy(res[:], acc[:])
+                rows.append(res)
+            return rows
+
+        offs_t = load_list(offs, "offs_t")
+        x_rows = xT.rearrange("(p j) c -> p j c", j=PACK)
+        x_raw = []
+        for j in range(PACK):
+            plane = keep.tile([P, T], F32, name="x_raw%d" % j)
+            nc.sync.dma_start(plane[:], x_rows[:, j, :])
+            x_raw.append(plane)
+        w1_raw = load_weight(w1, 4, "w1")
+        cen_t = load_list(cen, "cen_t")
+        w3_raw = load_weight(w3, 2, "w3")
+        pos_t = [load_list(pos1, "pos1_t"), load_list(pos2, "pos2_t")]
+        w2_raw = load_weight(w2, 2, "w2")
+
+        picked = keep.tile([P, PACK, S], BF16, name="picked")
+        for j in range(PACK):
+            nc.vector.tensor_copy(picked[:, j, :], x_raw[j][:].indirect(offs_t[:]))
+        woven = keep.tile([P, S, PACK], BF16, name="woven", align_bytes=64)
+        nc.vector.tensor_copy(
+            woven[:].rearrange("p (c i) j -> p c j i", i=PACK),
+            picked[:].rearrange("p j (c i) -> p c j i", i=PACK),
+        )
+        xq = quantize(woven[:].rearrange("p c j -> p (c j)"), S, "x")
+
+        flat = "p t m j -> p (t m j)"
+        w1_dealt = deal_weight(w1_raw, [nc.scalar.copy] * 4, "w1")
+        w1q = quantize(w1_dealt[:].rearrange(flat), N, "w1", calls=2)
+        w3_dealt = deal_weight(w3_raw, [nc.scalar.copy, nc.vector.tensor_copy], "w3")
+        g = product(w1q, xq, "g")
+        w3q = quantize(w3_dealt[:].rearrange(flat), N, "w3")
+        h = product(w3q, xq, "h")
+
+        gc = keep.tile([P, PACK, V], F32, name="gc")
+        for t in range(PACK):
+            nc.vector.tensor_copy(gc[:, t, :], g[t][:].indirect(cen_t[:]))
+
+        w2_dealt = deal_weight(w2_raw, [nc.scalar.copy] * 2, "w2")
+        scaled = []
+        for t in range(PACK):
+            tag = "w2_dealt" if t == 2 else "scaled%d" % t
+            scaled.append(keep.tile([P, 2, V], F32, name="scaled%d" % t, tag=tag, align_bytes=64))
+            for d in range(2):
+                nc.vector.tensor_tensor(scaled[t][:, d, :], h[t][:].indirect(pos_t[d][:]), gc[:, t, :], MULT)
+            if t == 1:
+                w2q = quantize(w2_dealt[:].rearrange(flat), N, "w2")
+                s = product(w2q, xq, "s")
+
+        sc = keep.tile([P, PACK, V], F32, name="sc")
+        shifted = keep.tile([P, PACK, 2, V], F32, name="shifted")
+        second = keep.tile([P, PACK, V], F32, name="second")
+        y = keep.tile([P, PACK, V], F32, name="y")
+        out_rows = out_0.rearrange("(p t) v -> p t v", t=PACK)
+
+        def finish(t):
+            nc.vector.scalar_tensor_tensor(y[:, t, :], shifted[:, t, 0, :], 0.0, second[:, t, :], MAX, ADD)
+            nc.sync.dma_start(out_rows[:, t, :], y[:, t, :])
+
+        for t in range(PACK):
+            nc.vector.tensor_copy(sc[:, t, :], s[t][:].indirect(cen_t[:]))
+            if t > 0:
+                finish(t - 1)
+            nc.vector.tensor_tensor(
+                shifted[:, t, :, :], scaled[t][:], sc[:, t : t + 1, :].broadcast_to([P, 2, V]), ADD
+            )
+            nc.scalar.activation(second[:, t, :], shifted[:, t, 1, :], RELU)
+        finish(PACK - 1)
+
+        y_woven = keep.tile([P, V, PACK], BF16, name="y_woven", align_bytes=64)
+        nc.vector.tensor_copy(
+            y_woven[:].rearrange("p (c i) t -> p c t i", i=PACK),
+            y[:].rearrange("p t (c i) -> p c t i", i=PACK),
+        )
+        yq = quantize(y_woven[:].rearrange("p c t -> p (c t)"), V, "y")
+        nc.sync.dma_start(out_1[0].rearrange("p c r -> p (c r)").bitcast(I32), yq[0][:].bitcast(I32))
+        for q in range(4):
+            queue = nc.scalar if q % 2 else nc.sync
+            queue.dma_start(out_2[0, 4 * q : 4 * q + 4, :].bitcast(I32), yq[1][32 * q : 32 * q + 4, :].bitcast(I32))

@@ -1,6 +1,7 @@
 from contextlib import ExitStack
 
 import concourse.mybir as mybir
+from concourse.masks import make_identity
 
 K, T, S, V, N = 512, 1024, 512, 256, 512
 FLOPS = 3 * 2 * K * N * S
@@ -27,63 +28,67 @@ def tile_picked_filmg_relu_lo_kernel(
     nc = tc.nc
     with ExitStack() as ctx:
         keep = ctx.enter_context(tc.tile_pool(name="keep", bufs=1))
-        psum = ctx.enter_context(tc.psum_pool(name="psum", bufs=8))
+        psum = ctx.enter_context(tc.psum_pool(name="psum", bufs=1))
 
         def load_list(src, name):
             tile = keep.tile([P, src.shape[1]], U16, name=name)
             nc.sync.dma_start(tile[:], src)
             return tile
 
-        def load_weight(w, pieces, name):
-            width = N // pieces
-            rows = w.rearrange("(p j) c -> p j c", j=PACK)
-            raws = []
-            for i in range(pieces):
-                raw = keep.tile([P, PACK, width], F32, name="%s_raw%d" % (name, i))
-                nc.sync.dma_start(raw[:], rows[:, :, i * width : (i + 1) * width])
-                raws.append(raw)
-            return raws
+        def load_rows(w, j0, j1, name):
+            raw = keep.tile([P, j1 - j0, w.shape[1]], F32, name=name)
+            nc.sync.dma_start(raw[:], w.rearrange("(p j) c -> p j c", j=PACK)[:, j0:j1, :])
+            return raw
 
-        def deal_weight(raws, copies, name):
-            dealt = keep.tile([P, PACK, P, PACK], BF16, name=name + "_dealt", align_bytes=64)
-            ms = P // len(raws)
-            for i, raw in enumerate(raws):
-                copies[i](
-                    dealt[:, :, i * ms : (i + 1) * ms, :].rearrange("p t m j -> p m j t"),
-                    raw[:].rearrange("p j (m t) -> p m j t", t=PACK),
-                )
-            return dealt
+        def load_cols(w, u, name):
+            raw = keep.tile([P, PACK, N // 2], F32, name=name, align_bytes=64)
+            nc.sync.dma_start(raw[:], w.rearrange("(p j) c -> p j c", j=PACK)[:, :, u * 256 : (u + 1) * 256])
+            return raw
 
-        def quantize(src, cols, name, calls=1):
+        def deal_half(copy, dealt, raw, u):
+            copy(
+                dealt[:, :, u * 64 : (u + 1) * 64, :].rearrange("p t m j -> p m j t"),
+                raw[:].rearrange("p j (m t) -> p m j t", t=PACK),
+            )
+
+        def dealt_tile(name):
+            return keep.tile([P, PACK, P, PACK], BF16, name=name, align_bytes=64)
+
+        def deal(copy, dealt, raw, ms, js):
+            copy(
+                dealt[:, :, ms, js].rearrange("p t m j -> p m j t"),
+                raw[:].rearrange("p j (m t) -> p m j t", t=PACK)[:, ms, :, :],
+            )
+
+        def mx_tiles(cols, name):
             codes = keep.tile([P, cols], U32, name=name + "_codes", align_bytes=64)
             scales = keep.tile([P, cols], U8, name=name + "_scales", align_bytes=64)
-            step = cols // calls
-            for i in range(calls):
-                nc.vector.quantize_mx(
-                    out=codes[:, i * step : (i + 1) * step].bitcast(FP8X4),
-                    scales=scales[:, i * step : (i + 1) * step],
-                    in_=src[:, i * step * PACK : (i + 1) * step * PACK],
-                )
             return codes, scales
 
-        def product(wq, xq, name):
-            rows = []
-            for t in range(PACK):
-                acc = psum.tile([P, S], F32, name="acc")
-                cols = slice(t * P, (t + 1) * P)
-                nc.tensor.matmul_mx(
-                    out=acc[:],
-                    lhsT=wq[0][:, cols].bitcast(FP8X4),
-                    lhsT_scale=wq[1][:, cols],
-                    rhs=xq[0][:].bitcast(FP8X4),
-                    rhs_scale=xq[1][:],
-                    start=True,
-                    stop=True,
-                )
-                res = keep.tile([P, S], F32, name="%s%d" % (name, t))
-                nc.scalar.copy(res[:], acc[:])
-                rows.append(res)
-            return rows
+        def quantize(dst, src, c0, c1):
+            nc.vector.quantize_mx(
+                out=dst[0][:, c0:c1].bitcast(FP8X4), scales=dst[1][:, c0:c1], in_=src[:, c0 * PACK : c1 * PACK]
+            )
+
+        def product(wq, xq, t, name, bank, tag=None):
+            acc = psum.tile([P, S], F32, name="acc", tag="bank%d" % bank)
+            cols = slice(t * P, (t + 1) * P)
+            nc.tensor.matmul_mx(
+                out=acc[:],
+                lhsT=wq[0][:, cols].bitcast(FP8X4),
+                lhsT_scale=wq[1][:, cols],
+                rhs=xq[0][:].bitcast(FP8X4),
+                rhs_scale=xq[1][:],
+                start=True,
+                stop=True,
+            )
+            res = keep.tile([P, S], F32, name="%s%d" % (name, t), tag=tag or "%s%d" % (name, t), align_bytes=64)
+            nc.scalar.copy(res[:], acc[:])
+            return res
+
+        every, all_m = slice(0, PACK), slice(0, P)
+        low, high = slice(0, 2), slice(2, 4)
+        flat = "p t m j -> p (t m j)"
 
         offs_t = load_list(offs, "offs_t")
         x_rows = xT.rearrange("(p j) c -> p j c", j=PACK)
@@ -92,71 +97,119 @@ def tile_picked_filmg_relu_lo_kernel(
             plane = keep.tile([P, T], F32, name="x_raw%d" % j)
             nc.sync.dma_start(plane[:], x_rows[:, j, :])
             x_raw.append(plane)
-        w1_raw = load_weight(w1, 4, "w1")
+        w1_raw = [load_cols(w1, u, "w1_raw%d" % u) for u in range(2)]
+        w3_raw = [load_cols(w3, u, "w3_raw%d" % u) for u in range(2)]
         cen_t = load_list(cen, "cen_t")
-        w3_raw = load_weight(w3, 2, "w3")
         pos_t = [load_list(pos1, "pos1_t"), load_list(pos2, "pos2_t")]
-        w2_raw = load_weight(w2, 2, "w2")
+        w2_raw = [load_cols(w2, u, "w2_raw%d" % u) for u in range(2)]
+        ident = keep.tile([P, P], F32, name="ident")
+        make_identity(nc, ident[:])
 
-        picked = keep.tile([P, PACK, S], BF16, name="picked")
-        for j in range(PACK):
-            nc.vector.tensor_copy(picked[:, j, :], x_raw[j][:].indirect(offs_t[:]))
+        picked = [keep.tile([P, 2, S], BF16, name="picked%d" % u) for u in range(2)]
         woven = keep.tile([P, S, PACK], BF16, name="woven", align_bytes=64)
-        nc.vector.tensor_copy(
-            woven[:].rearrange("p (c i) j -> p c j i", i=PACK),
-            picked[:].rearrange("p j (c i) -> p c j i", i=PACK),
-        )
-        xq = quantize(woven[:].rearrange("p c j -> p (c j)"), S, "x")
+        for j in range(PACK):
+            nc.vector.tensor_copy(picked[j // 2][:, j % 2, :], x_raw[j][:].indirect(offs_t[:]))
+        nc.scalar.copy(woven[:, :, low], picked[0][:].rearrange("p j c -> p c j"))
+        nc.vector.tensor_copy(woven[:, :, high], picked[1][:].rearrange("p j c -> p c j"))
+        xq = mx_tiles(S, "x")
+        quantize(xq, woven[:].rearrange("p c j -> p (c j)"), 0, S)
 
-        flat = "p t m j -> p (t m j)"
-        w1_dealt = deal_weight(w1_raw, [nc.scalar.copy] * 4, "w1")
-        w1q = quantize(w1_dealt[:].rearrange(flat), N, "w1", calls=2)
-        w3_dealt = deal_weight(w3_raw, [nc.scalar.copy, nc.vector.tensor_copy], "w3")
-        g = product(w1q, xq, "g")
-        w3q = quantize(w3_dealt[:].rearrange(flat), N, "w3")
-        h = product(w3q, xq, "h")
+        w1_dealt = dealt_tile("w1_dealt")
+        w1q = mx_tiles(N, "w1")
+        for u in range(2):
+            deal_half(nc.scalar.copy, w1_dealt, w1_raw[u], u)
+        quantize(w1q, w1_dealt[:].rearrange(flat), 0, P)
+        quantize(w1q, w1_dealt[:].rearrange(flat), P, 2 * P)
+        quantize(w1q, w1_dealt[:].rearrange(flat), 2 * P, N)
+        w3_dealt = dealt_tile("w3_dealt")
+        deal_half(nc.scalar.copy, w3_dealt, w3_raw[0], 0)
+        g = [product(w1q, xq, t, "g", t) for t in range(PACK)]
+        deal_half(nc.vector.tensor_copy, w3_dealt, w3_raw[1], 1)
+        w3q = mx_tiles(N, "w3")
+        quantize(w3q, w3_dealt[:].rearrange(flat), 0, N)
 
         gc = keep.tile([P, PACK, V], F32, name="gc")
         for t in range(PACK):
             nc.vector.tensor_copy(gc[:, t, :], g[t][:].indirect(cen_t[:]))
 
-        w2_dealt = deal_weight(w2_raw, [nc.scalar.copy] * 2, "w2")
+        w2_dealt = dealt_tile("w2_dealt")
+        h = []
+        for u in range(2):
+            deal_half(nc.scalar.copy, w2_dealt, w2_raw[u], u)
+            h.append(product(w3q, xq, u, "h", 4 + u, tag="w2_raw%d" % u))
+        w2q = mx_tiles(N, "w2")
         scaled = []
-        for t in range(PACK):
-            tag = "w2_dealt" if t == 2 else "scaled%d" % t
-            scaled.append(keep.tile([P, 2, V], F32, name="scaled%d" % t, tag=tag, align_bytes=64))
+        tags = ["scaled0", "w2_dealt", "s0", "s1"]
+
+        def scale(t):
+            scaled.append(keep.tile([P, 2, V], F32, name="scaled%d" % t, tag=tags[t], align_bytes=64))
             for d in range(2):
                 nc.vector.tensor_tensor(scaled[t][:, d, :], h[t][:].indirect(pos_t[d][:]), gc[:, t, :], MULT)
-            if t == 1:
-                w2q = quantize(w2_dealt[:].rearrange(flat), N, "w2")
-                s = product(w2q, xq, "s")
 
-        sc = keep.tile([P, PACK, V], F32, name="sc")
-        shifted = keep.tile([P, PACK, 2, V], F32, name="shifted")
-        second = keep.tile([P, PACK, V], F32, name="second")
-        y = keep.tile([P, PACK, V], F32, name="y")
+        scale(0)
+        quantize(w2q, w2_dealt[:].rearrange(flat), 0, N)
+        s = [product(w2q, xq, t, "s", 6 + t) for t in range(2)]
+        h.extend(product(w3q, xq, t, "h", 4 + t) for t in range(2, PACK))
+        s.extend(product(w2q, xq, t, "s", t - 2) for t in range(2, PACK))
+
+        sc = [keep.tile([P, V], F32, name="sc%d" % t) for t in range(PACK)]
+        y = [keep.tile([P, 2, V], F32, name="y%d" % u) for u in range(2)]
+        y_woven = keep.tile([P, V, PACK], BF16, name="y_woven", align_bytes=64)
         out_rows = out_0.rearrange("(p t) v -> p t v", t=PACK)
 
-        def finish(t):
-            nc.vector.scalar_tensor_tensor(y[:, t, :], shifted[:, t, 0, :], 0.0, second[:, t, :], MAX, ADD)
-            nc.sync.dma_start(out_rows[:, t, :], y[:, t, :])
+        def fetch_shift(t):
+            nc.vector.tensor_copy(sc[t][:], s[t][:].indirect(cen_t[:]))
 
-        for t in range(PACK):
-            nc.vector.tensor_copy(sc[:, t, :], s[t][:].indirect(cen_t[:]))
-            if t > 0:
-                finish(t - 1)
-            nc.vector.tensor_tensor(
-                shifted[:, t, :, :], scaled[t][:], sc[:, t : t + 1, :].broadcast_to([P, 2, V]), ADD
-            )
-            nc.scalar.activation(second[:, t, :], shifted[:, t, 1, :], RELU)
-        finish(PACK - 1)
+        def shift(t):
+            shifted = keep.tile([P, 2, V], F32, name="shifted%d" % t)
+            second = keep.tile([P, V], F32, name="second%d" % t)
+            nc.vector.tensor_tensor(shifted[:], scaled[t][:], sc[t][:].unsqueeze(1).broadcast_to([P, 2, V]), ADD)
+            nc.vector.tensor_scalar_max(second[:], shifted[:, 1, :], 0.0)
+            return shifted, second
 
-        y_woven = keep.tile([P, V, PACK], BF16, name="y_woven", align_bytes=64)
-        nc.vector.tensor_copy(
-            y_woven[:].rearrange("p (c i) t -> p c t i", i=PACK),
-            y[:].rearrange("p t (c i) -> p c t i", i=PACK),
-        )
-        yq = quantize(y_woven[:].rearrange("p c t -> p (c t)"), V, "y")
+        def finish(t, pair):
+            nc.vector.scalar_tensor_tensor(y[t // 2][:, t % 2, :], pair[0][:, 0, :], 0.0, pair[1][:], MAX, ADD)
+            nc.sync.dma_start(out_rows[:, t, :], y[t // 2][:, t % 2, :])
+
+        def shift_on_tensor(t):
+            turned = psum.tile([P, 4, P], F32, name="turned", tag="bank%d" % (2 + t))
+            for d in range(2):
+                for half in range(2):
+                    cols = slice(half * P, (half + 1) * P)
+                    dst = turned[:, 2 * d + half, :]
+                    nc.tensor.matmul(dst, scaled[t][:, d, cols], ident[:], start=True, stop=False, is_transpose=True)
+                    nc.tensor.matmul(dst, sc[t][:, cols], ident[:], start=False, stop=True, is_transpose=True)
+            rect = keep.tile([P, 4, P], F32, name="rect%d" % t)
+            nc.scalar.activation(rect[:], turned[:], RELU)
+            return rect
+
+        def finish_on_tensor(t, rect):
+            back = psum.tile([P, 4, P], F32, name="back", tag="bank%d" % (4 + t))
+            for half in range(2):
+                nc.tensor.matmul(back[:, half, :], rect[:, half, :], ident[:], start=True, stop=False, is_transpose=True)
+                nc.tensor.matmul(back[:, half, :], rect[:, 2 + half, :], ident[:], start=False, stop=True, is_transpose=True)
+            nc.scalar.copy(y[t // 2][:, t % 2, :], back[:, 0:2, :].rearrange("p h v -> p (h v)"))
+            nc.sync.dma_start(out_rows[:, t, :], y[t // 2][:, t % 2, :])
+
+        scale(1)
+        rects = []
+        for t in range(2):
+            fetch_shift(t)
+            rects.append(shift_on_tensor(t))
+        for t in range(2):
+            finish_on_tensor(t, rects[t])
+        scale(2)
+        scale(3)
+        fetch_shift(2)
+        fetch_shift(3)
+        pairs = [shift(2), shift(3)]
+        finish(2, pairs[0])
+        finish(3, pairs[1])
+
+        nc.scalar.copy(y_woven[:, :, low], y[0][:].rearrange("p t c -> p c t"))
+        nc.vector.tensor_copy(y_woven[:, :, high], y[1][:].rearrange("p t c -> p c t"))
+        yq = mx_tiles(V, "y")
+        quantize(yq, y_woven[:].rearrange("p c t -> p (c t)"), 0, V)
         nc.sync.dma_start(out_1[0].rearrange("p c r -> p (c r)").bitcast(I32), yq[0][:].bitcast(I32))
         for q in range(4):
             queue = nc.scalar if q % 2 else nc.sync

@@ -90,13 +90,14 @@ def tile_picked_filmg_relu_lo_kernel(
         low, high = slice(0, 2), slice(2, 4)
         flat = "p t m j -> p (t m j)"
 
-        offs_t = load_list(offs, "offs_t")
         x_rows = xT.rearrange("(p j) c -> p j c", j=PACK)
         x_raw = []
         for j in range(PACK):
             plane = keep.tile([P, T], F32, name="x_raw%d" % j)
             nc.sync.dma_start(plane[:], x_rows[:, j, :])
             x_raw.append(plane)
+            if j == 0:
+                offs_t = load_list(offs, "offs_t")
         w1_raw = [load_cols(w1, u, "w1_raw%d" % u) for u in range(2)]
         w3_raw = [load_cols(w3, u, "w3_raw%d" % u) for u in range(2)]
         cen_t = load_list(cen, "cen_t")
@@ -138,18 +139,24 @@ def tile_picked_filmg_relu_lo_kernel(
             deal_half(nc.scalar.copy, w2_dealt, w2_raw[u], u)
             h.append(product(w3q, xq, u, "h", 4 + u, tag="w2_raw%d" % u))
         w2q = mx_tiles(N, "w2")
-        scaled = []
-        tags = ["scaled0", "w2_dealt", "s0", "s1"]
+        scaled = {}
+        tags = [None, (None, None), ("s0", "s1"), ("s2", "s3")]
 
         def scale(t):
-            scaled.append(keep.tile([P, 2, V], F32, name="scaled%d" % t, tag=tags[t], align_bytes=64))
             for d in range(2):
-                nc.vector.tensor_tensor(scaled[t][:, d, :], h[t][:].indirect(pos_t[d][:]), gc[:, t, :], MULT)
+                scale_one(t, d, tags[t][d])
 
-        scale(0)
+        def scale_one(t, d, tag):
+            name = "scaled%d_%d" % (t, d)
+            scaled[t, d] = keep.tile([P, V], F32, name=name, tag=tag or name, align_bytes=64)
+            nc.vector.tensor_tensor(scaled[t, d][:], h[t][:].indirect(pos_t[d][:]), gc[:, t, :], MULT)
+
+        scale_one(0, 0, None)
         quantize(w2q, w2_dealt[:].rearrange(flat), 0, N)
+        scale_one(0, 1, "w2_dealt")
+        h.append(product(w3q, xq, 2, "h", 5))
         s = [product(w2q, xq, t, "s", 6 + t) for t in range(2)]
-        h.extend(product(w3q, xq, t, "h", 4 + t) for t in range(2, PACK))
+        h.append(product(w3q, xq, 3, "h", 5))
         s.extend(product(w2q, xq, t, "s", t - 2) for t in range(2, PACK))
 
         sc = [keep.tile([P, V], F32, name="sc%d" % t) for t in range(PACK)]
@@ -160,31 +167,20 @@ def tile_picked_filmg_relu_lo_kernel(
         def fetch_shift(t):
             nc.vector.tensor_copy(sc[t][:], s[t][:].indirect(cen_t[:]))
 
-        def shift(t):
-            shifted = keep.tile([P, 2, V], F32, name="shifted%d" % t)
-            second = keep.tile([P, V], F32, name="second%d" % t)
-            nc.vector.tensor_tensor(shifted[:], scaled[t][:], sc[t][:].unsqueeze(1).broadcast_to([P, 2, V]), ADD)
-            nc.vector.tensor_scalar_max(second[:], shifted[:, 1, :], 0.0)
-            return shifted, second
-
-        def finish(t, pair):
-            nc.vector.scalar_tensor_tensor(y[t // 2][:, t % 2, :], pair[0][:, 0, :], 0.0, pair[1][:], MAX, ADD)
-            nc.sync.dma_start(out_rows[:, t, :], y[t // 2][:, t % 2, :])
-
         def shift_on_tensor(t):
-            turned = psum.tile([P, 4, P], F32, name="turned", tag="bank%d" % (2 + t))
+            turned = psum.tile([P, 4, P], F32, name="turned", tag="bank%d" % (2, 3, 3)[t])
             for d in range(2):
                 for half in range(2):
                     cols = slice(half * P, (half + 1) * P)
                     dst = turned[:, 2 * d + half, :]
-                    nc.tensor.matmul(dst, scaled[t][:, d, cols], ident[:], start=True, stop=False, is_transpose=True)
+                    nc.tensor.matmul(dst, scaled[t, d][:, cols], ident[:], start=True, stop=False, is_transpose=True)
                     nc.tensor.matmul(dst, sc[t][:, cols], ident[:], start=False, stop=True, is_transpose=True)
             rect = keep.tile([P, 4, P], F32, name="rect%d" % t)
             nc.scalar.activation(rect[:], turned[:], RELU)
             return rect
 
         def finish_on_tensor(t, rect):
-            back = psum.tile([P, 4, P], F32, name="back", tag="bank%d" % (4 + t))
+            back = psum.tile([P, 4, P], F32, name="back", tag="bank%d" % (4, 5, 6)[t])
             for half in range(2):
                 nc.tensor.matmul(back[:, half, :], rect[:, half, :], ident[:], start=True, stop=False, is_transpose=True)
                 nc.tensor.matmul(back[:, half, :], rect[:, 2 + half, :], ident[:], start=False, stop=True, is_transpose=True)
@@ -199,12 +195,17 @@ def tile_picked_filmg_relu_lo_kernel(
         for t in range(2):
             finish_on_tensor(t, rects[t])
         scale(2)
-        scale(3)
         fetch_shift(2)
+        finish_on_tensor(2, shift_on_tensor(2))
         fetch_shift(3)
-        pairs = [shift(2), shift(3)]
-        finish(2, pairs[0])
-        finish(3, pairs[1])
+        scale(3)
+        shifted = keep.tile([P, 2, V], F32, name="shifted")
+        for d in range(2):
+            nc.vector.tensor_tensor(shifted[:, d, :], scaled[3, d][:], sc[3][:], ADD)
+        first = keep.tile([P, V], F32, name="first")
+        nc.vector.tensor_scalar_max(first[:], shifted[:, 0, :], 0.0)
+        nc.vector.scalar_tensor_tensor(y[1][:, 1, :], shifted[:, 1, :], 0.0, first[:], MAX, ADD)
+        nc.sync.dma_start(out_rows[:, 3, :], y[1][:, 1, :])
 
         nc.scalar.copy(y_woven[:, :, low], y[0][:].rearrange("p t c -> p c t"))
         nc.vector.tensor_copy(y_woven[:, :, high], y[1][:].rearrange("p t c -> p c t"))

@@ -20,6 +20,9 @@ RELU = mybir.ActivationFunctionType.Relu
 
 P = 128
 PACK = 4
+NEIGHBOURS = 2
+HALVES = 2
+ALIGN = 64
 
 
 def tile_picked_filmg_relu_lo_kernel(
@@ -35,34 +38,29 @@ def tile_picked_filmg_relu_lo_kernel(
             nc.sync.dma_start(tile[:], src)
             return tile
 
-        def load_rows(w, j0, j1, name):
-            raw = keep.tile([P, j1 - j0, w.shape[1]], F32, name=name)
-            nc.sync.dma_start(raw[:], w.rearrange("(p j) c -> p j c", j=PACK)[:, j0:j1, :])
-            return raw
+        def load_weight(w, name):
+            rows = w.rearrange("(p j) c -> p j c", j=PACK)
+            width = N // HALVES
+            halves = []
+            for u in range(HALVES):
+                raw = keep.tile([P, PACK, width], F32, name="%s_raw%d" % (name, u), align_bytes=ALIGN)
+                nc.sync.dma_start(raw[:], rows[:, :, u * width : (u + 1) * width])
+                halves.append(raw)
+            return halves
 
-        def load_cols(w, u, name):
-            raw = keep.tile([P, PACK, N // 2], F32, name=name, align_bytes=64)
-            nc.sync.dma_start(raw[:], w.rearrange("(p j) c -> p j c", j=PACK)[:, :, u * 256 : (u + 1) * 256])
-            return raw
+        def dealt_tile(name):
+            return keep.tile([P, PACK, P, PACK], BF16, name=name, align_bytes=ALIGN)
 
         def deal_half(copy, dealt, raw, u):
+            count = P // HALVES
             copy(
-                dealt[:, :, u * 64 : (u + 1) * 64, :].rearrange("p t m j -> p m j t"),
+                dealt[:, :, u * count : (u + 1) * count, :].rearrange("p t m j -> p m j t"),
                 raw[:].rearrange("p j (m t) -> p m j t", t=PACK),
             )
 
-        def dealt_tile(name):
-            return keep.tile([P, PACK, P, PACK], BF16, name=name, align_bytes=64)
-
-        def deal(copy, dealt, raw, ms, js):
-            copy(
-                dealt[:, :, ms, js].rearrange("p t m j -> p m j t"),
-                raw[:].rearrange("p j (m t) -> p m j t", t=PACK)[:, ms, :, :],
-            )
-
         def mx_tiles(cols, name):
-            codes = keep.tile([P, cols], U32, name=name + "_codes", align_bytes=64)
-            scales = keep.tile([P, cols], U8, name=name + "_scales", align_bytes=64)
+            codes = keep.tile([P, cols], U32, name=name + "_codes", align_bytes=ALIGN)
+            scales = keep.tile([P, cols], U8, name=name + "_scales", align_bytes=ALIGN)
             return codes, scales
 
         def quantize(dst, src, c0, c1):
@@ -70,7 +68,7 @@ def tile_picked_filmg_relu_lo_kernel(
                 out=dst[0][:, c0:c1].bitcast(FP8X4), scales=dst[1][:, c0:c1], in_=src[:, c0 * PACK : c1 * PACK]
             )
 
-        def product(wq, xq, t, name, bank, tag=None):
+        def product(wq, t, name, bank, tag=None):
             acc = psum.tile([P, S], F32, name="acc", tag="bank%d" % bank)
             cols = slice(t * P, (t + 1) * P)
             nc.tensor.matmul_mx(
@@ -82,136 +80,139 @@ def tile_picked_filmg_relu_lo_kernel(
                 start=True,
                 stop=True,
             )
-            res = keep.tile([P, S], F32, name="%s%d" % (name, t), tag=tag or "%s%d" % (name, t), align_bytes=64)
-            nc.scalar.copy(res[:], acc[:])
-            return res
+            own = "%s%d" % (name, t)
+            rows = keep.tile([P, S], F32, name=own, tag=tag or own, align_bytes=ALIGN)
+            nc.scalar.copy(rows[:], acc[:])
+            return rows
 
-        every, all_m = slice(0, PACK), slice(0, P)
+        def add_transposed(dst, first, second):
+            nc.tensor.matmul(dst, first, ident[:], start=True, stop=False, is_transpose=True)
+            nc.tensor.matmul(dst, second, ident[:], start=False, stop=True, is_transpose=True)
+
         low, high = slice(0, 2), slice(2, 4)
         flat = "p t m j -> p (t m j)"
 
         x_rows = xT.rearrange("(p j) c -> p j c", j=PACK)
-        x_raw = []
-        for j in range(PACK):
-            plane = keep.tile([P, T], F32, name="x_raw%d" % j)
-            nc.sync.dma_start(plane[:], x_rows[:, j, :])
-            x_raw.append(plane)
-            if j == 0:
-                offs_t = load_list(offs, "offs_t")
-        w1_raw = [load_cols(w1, u, "w1_raw%d" % u) for u in range(2)]
-        w3_raw = [load_cols(w3, u, "w3_raw%d" % u) for u in range(2)]
+        planes = [keep.tile([P, T], F32, name="plane%d" % j) for j in range(PACK)]
+        nc.sync.dma_start(planes[0][:], x_rows[:, 0, :])
+        offs_t = load_list(offs, "offs_t")
+        for j in range(1, PACK):
+            nc.sync.dma_start(planes[j][:], x_rows[:, j, :])
+        w1_raw = load_weight(w1, "w1")
+        w3_raw = load_weight(w3, "w3")
         cen_t = load_list(cen, "cen_t")
         pos_t = [load_list(pos1, "pos1_t"), load_list(pos2, "pos2_t")]
-        w2_raw = [load_cols(w2, u, "w2_raw%d" % u) for u in range(2)]
+        w2_raw = load_weight(w2, "w2")
         ident = keep.tile([P, P], F32, name="ident")
         make_identity(nc, ident[:])
 
         picked = [keep.tile([P, 2, S], BF16, name="picked%d" % u) for u in range(2)]
-        woven = keep.tile([P, S, PACK], BF16, name="woven", align_bytes=64)
+        x_woven = keep.tile([P, S, PACK], BF16, name="x_woven", align_bytes=ALIGN)
         for j in range(PACK):
-            nc.vector.tensor_copy(picked[j // 2][:, j % 2, :], x_raw[j][:].indirect(offs_t[:]))
-        nc.scalar.copy(woven[:, :, low], picked[0][:].rearrange("p j c -> p c j"))
-        nc.vector.tensor_copy(woven[:, :, high], picked[1][:].rearrange("p j c -> p c j"))
+            nc.vector.tensor_copy(picked[j // 2][:, j % 2, :], planes[j][:].indirect(offs_t[:]))
+        nc.scalar.copy(x_woven[:, :, low], picked[0][:].rearrange("p j c -> p c j"))
+        nc.vector.tensor_copy(x_woven[:, :, high], picked[1][:].rearrange("p j c -> p c j"))
         xq = mx_tiles(S, "x")
-        quantize(xq, woven[:].rearrange("p c j -> p (c j)"), 0, S)
+        quantize(xq, x_woven[:].rearrange("p c j -> p (c j)"), 0, S)
 
         w1_dealt = dealt_tile("w1_dealt")
         w1q = mx_tiles(N, "w1")
-        for u in range(2):
+        for u in range(HALVES):
             deal_half(nc.scalar.copy, w1_dealt, w1_raw[u], u)
-        quantize(w1q, w1_dealt[:].rearrange(flat), 0, P)
-        quantize(w1q, w1_dealt[:].rearrange(flat), P, 2 * P)
-        quantize(w1q, w1_dealt[:].rearrange(flat), 2 * P, N)
+        for c0, c1 in ((0, P), (P, 2 * P), (2 * P, N)):
+            quantize(w1q, w1_dealt[:].rearrange(flat), c0, c1)
         w3_dealt = dealt_tile("w3_dealt")
         deal_half(nc.scalar.copy, w3_dealt, w3_raw[0], 0)
-        g = [product(w1q, xq, t, "g", t) for t in range(PACK)]
+        g = [product(w1q, t, "g", bank=t) for t in range(PACK)]
         deal_half(nc.vector.tensor_copy, w3_dealt, w3_raw[1], 1)
         w3q = mx_tiles(N, "w3")
         quantize(w3q, w3_dealt[:].rearrange(flat), 0, N)
 
-        gc = keep.tile([P, PACK, V], F32, name="gc")
+        gain = keep.tile([P, PACK, V], F32, name="gain")
         for t in range(PACK):
-            nc.vector.tensor_copy(gc[:, t, :], g[t][:].indirect(cen_t[:]))
+            nc.vector.tensor_copy(gain[:, t, :], g[t][:].indirect(cen_t[:]))
 
         w2_dealt = dealt_tile("w2_dealt")
         h = []
-        for u in range(2):
+        for u in range(HALVES):
             deal_half(nc.scalar.copy, w2_dealt, w2_raw[u], u)
-            h.append(product(w3q, xq, u, "h", 4 + u, tag="w2_raw%d" % u))
-        w2q = mx_tiles(N, "w2")
+            h.append(product(w3q, u, "h", bank=4 + u, tag="w2_raw%d" % u))
+
         scaled = {}
-        tags = [None, (None, None), ("s0", "s1"), ("s2", "s3")]
 
-        def scale(t):
-            for d in range(2):
-                scale_one(t, d, tags[t][d])
+        def scale(t, d, tag=None):
+            own = "scaled%d_%d" % (t, d)
+            scaled[t, d] = keep.tile([P, V], F32, name=own, tag=tag or own, align_bytes=ALIGN)
+            nc.vector.tensor_tensor(scaled[t, d][:], h[t][:].indirect(pos_t[d][:]), gain[:, t, :], MULT)
 
-        def scale_one(t, d, tag):
-            name = "scaled%d_%d" % (t, d)
-            scaled[t, d] = keep.tile([P, V], F32, name=name, tag=tag or name, align_bytes=64)
-            nc.vector.tensor_tensor(scaled[t, d][:], h[t][:].indirect(pos_t[d][:]), gc[:, t, :], MULT)
-
-        scale_one(0, 0, None)
+        w2q = mx_tiles(N, "w2")
+        scale(0, 0)
         quantize(w2q, w2_dealt[:].rearrange(flat), 0, N)
-        scale_one(0, 1, "w2_dealt")
-        h.append(product(w3q, xq, 2, "h", 5))
-        s = [product(w2q, xq, t, "s", 6 + t) for t in range(2)]
-        h.append(product(w3q, xq, 3, "h", 5))
-        s.extend(product(w2q, xq, t, "s", t - 2) for t in range(2, PACK))
+        scale(0, 1, tag="w2_dealt")
+        h.append(product(w3q, 2, "h", bank=5))
+        s = [product(w2q, t, "s", bank=6 + t) for t in range(2)]
+        h.append(product(w3q, 3, "h", bank=5))
+        s.extend(product(w2q, t, "s", bank=t - 2) for t in range(2, PACK))
 
-        sc = [keep.tile([P, V], F32, name="sc%d" % t) for t in range(PACK)]
+        shift = [keep.tile([P, V], F32, name="shift%d" % t) for t in range(PACK)]
         y = [keep.tile([P, 2, V], F32, name="y%d" % u) for u in range(2)]
-        y_woven = keep.tile([P, V, PACK], BF16, name="y_woven", align_bytes=64)
         out_rows = out_0.rearrange("(p t) v -> p t v", t=PACK)
 
         def fetch_shift(t):
-            nc.vector.tensor_copy(sc[t][:], s[t][:].indirect(cen_t[:]))
+            nc.vector.tensor_copy(shift[t][:], s[t][:].indirect(cen_t[:]))
 
-        def shift_on_tensor(t):
-            turned = psum.tile([P, 4, P], F32, name="turned", tag="bank%d" % (2, 3, 3)[t])
-            for d in range(2):
-                for half in range(2):
-                    cols = slice(half * P, (half + 1) * P)
-                    dst = turned[:, 2 * d + half, :]
-                    nc.tensor.matmul(dst, scaled[t, d][:, cols], ident[:], start=True, stop=False, is_transpose=True)
-                    nc.tensor.matmul(dst, sc[t][:, cols], ident[:], start=False, stop=True, is_transpose=True)
-            rect = keep.tile([P, 4, P], F32, name="rect%d" % t)
+        def store(t):
+            nc.sync.dma_start(out_rows[:, t, :], y[t // 2][:, t % 2, :])
+
+        def relu_on_tensor(t):
+            turned = psum.tile([P, NEIGHBOURS, HALVES, P], F32, name="turned", tag="bank%d" % (2 + t))
+            for d in range(NEIGHBOURS):
+                for u in range(HALVES):
+                    cols = slice(u * P, (u + 1) * P)
+                    add_transposed(turned[:, d, u, :], scaled[t, d][:, cols], shift[t][:, cols])
+            rect = keep.tile([P, NEIGHBOURS, HALVES, P], F32, name="rect%d" % t)
             nc.scalar.activation(rect[:], turned[:], RELU)
             return rect
 
-        def finish_on_tensor(t, rect):
-            back = psum.tile([P, 4, P], F32, name="back", tag="bank%d" % (4, 5, 6)[t])
-            for half in range(2):
-                nc.tensor.matmul(back[:, half, :], rect[:, half, :], ident[:], start=True, stop=False, is_transpose=True)
-                nc.tensor.matmul(back[:, half, :], rect[:, 2 + half, :], ident[:], start=False, stop=True, is_transpose=True)
-            nc.scalar.copy(y[t // 2][:, t % 2, :], back[:, 0:2, :].rearrange("p h v -> p (h v)"))
-            nc.sync.dma_start(out_rows[:, t, :], y[t // 2][:, t % 2, :])
+        def sum_on_tensor(t, rect):
+            back = psum.tile([P, HALVES, P], F32, name="back", tag="bank%d" % (4 + t))
+            for u in range(HALVES):
+                add_transposed(back[:, u, :], rect[:, 0, u, :], rect[:, 1, u, :])
+            nc.scalar.copy(y[t // 2][:, t % 2, :], back[:].rearrange("p u v -> p (u v)"))
+            store(t)
 
-        scale(1)
+        def finish_on_vector(t):
+            shifted = keep.tile([P, NEIGHBOURS, V], F32, name="shifted%d" % t)
+            for d in range(NEIGHBOURS):
+                nc.vector.tensor_tensor(shifted[:, d, :], scaled[t, d][:], shift[t][:], ADD)
+            first = keep.tile([P, V], F32, name="first%d" % t)
+            nc.vector.tensor_scalar_max(first[:], shifted[:, 0, :], 0.0)
+            nc.vector.scalar_tensor_tensor(y[t // 2][:, t % 2, :], shifted[:, 1, :], 0.0, first[:], MAX, ADD)
+            store(t)
+
+        for d in range(NEIGHBOURS):
+            scale(1, d)
         rects = []
         for t in range(2):
             fetch_shift(t)
-            rects.append(shift_on_tensor(t))
+            rects.append(relu_on_tensor(t))
         for t in range(2):
-            finish_on_tensor(t, rects[t])
-        scale(2)
-        fetch_shift(2)
-        finish_on_tensor(2, shift_on_tensor(2))
-        fetch_shift(3)
-        scale(3)
-        shifted = keep.tile([P, 2, V], F32, name="shifted")
-        for d in range(2):
-            nc.vector.tensor_tensor(shifted[:, d, :], scaled[3, d][:], sc[3][:], ADD)
-        first = keep.tile([P, V], F32, name="first")
-        nc.vector.tensor_scalar_max(first[:], shifted[:, 0, :], 0.0)
-        nc.vector.scalar_tensor_tensor(y[1][:, 1, :], shifted[:, 1, :], 0.0, first[:], MAX, ADD)
-        nc.sync.dma_start(out_rows[:, 3, :], y[1][:, 1, :])
+            sum_on_tensor(t, rects[t])
+        for d in range(NEIGHBOURS):
+            scale(2, d, tag="s%d" % d)
+        for t in range(2, PACK):
+            fetch_shift(t)
+        for d in range(NEIGHBOURS):
+            scale(3, d, tag="s%d" % (2 + d))
+        for t in range(2, PACK):
+            finish_on_vector(t)
 
+        y_woven = keep.tile([P, V, PACK], BF16, name="y_woven", align_bytes=ALIGN)
         nc.scalar.copy(y_woven[:, :, low], y[0][:].rearrange("p t c -> p c t"))
         nc.vector.tensor_copy(y_woven[:, :, high], y[1][:].rearrange("p t c -> p c t"))
         yq = mx_tiles(V, "y")
         quantize(yq, y_woven[:].rearrange("p c t -> p (c t)"), 0, V)
         nc.sync.dma_start(out_1[0].rearrange("p c r -> p (c r)").bitcast(I32), yq[0][:].bitcast(I32))
-        for q in range(4):
+        for q in range(P // 32):
             queue = nc.scalar if q % 2 else nc.sync
             queue.dma_start(out_2[0, 4 * q : 4 * q + 4, :].bitcast(I32), yq[1][32 * q : 32 * q + 4, :].bitcast(I32))

from contextlib import ExitStack

import concourse.mybir as mybir
from concourse.masks import make_identity

K, T, S, V, N = 512, 1024, 512, 256, 512
FLOPS = 3 * 2 * K * N * S

F32 = mybir.dt.float32
BF16 = mybir.dt.bfloat16
I32 = mybir.dt.int32
U32 = mybir.dt.uint32
U16 = mybir.dt.uint16
U8 = mybir.dt.uint8
FP8X4 = mybir.dt.float8_e4m3fn_x4
MULT = mybir.AluOpType.mult
ADD = mybir.AluOpType.add
MAX = mybir.AluOpType.max
RELU = mybir.ActivationFunctionType.Relu

P = 128
PACK = 4
NEIGHBOURS = 2
HALVES = 2
ALIGN = 64


def tile_picked_filmg_relu_lo_kernel(
    tc, xT, w1, w2, w3, offs, cen, pos1, pos2, out_0, out_1, out_2
):
    nc = tc.nc
    with ExitStack() as ctx:
        keep = ctx.enter_context(tc.tile_pool(name="keep", bufs=1))
        psum = ctx.enter_context(tc.psum_pool(name="psum", bufs=1))

        def load_list(src, name):
            tile = keep.tile([P, src.shape[1]], U16, name=name)
            nc.sync.dma_start(tile[:], src)
            return tile

        def load_weight(w, name):
            rows = w.rearrange("(p j) c -> p j c", j=PACK)
            width = N // HALVES
            halves = []
            for u in range(HALVES):
                raw = keep.tile([P, PACK, width], F32, name="%s_raw%d" % (name, u), align_bytes=ALIGN)
                nc.sync.dma_start(raw[:], rows[:, :, u * width : (u + 1) * width])
                halves.append(raw)
            return halves

        def dealt_tile(name):
            return keep.tile([P, PACK, P, PACK], BF16, name=name, align_bytes=ALIGN)

        def deal_half(copy, dealt, raw, u):
            count = P // HALVES
            copy(
                dealt[:, :, u * count : (u + 1) * count, :].rearrange("p t m j -> p m j t"),
                raw[:].rearrange("p j (m t) -> p m j t", t=PACK),
            )

        def mx_tiles(cols, name):
            codes = keep.tile([P, cols], U32, name=name + "_codes", align_bytes=ALIGN)
            scales = keep.tile([P, cols], U8, name=name + "_scales", align_bytes=ALIGN)
            return codes, scales

        def quantize(dst, src, c0, c1):
            nc.vector.quantize_mx(
                out=dst[0][:, c0:c1].bitcast(FP8X4), scales=dst[1][:, c0:c1], in_=src[:, c0 * PACK : c1 * PACK]
            )

        def product(wq, t, name, bank, tag=None):
            acc = psum.tile([P, S], F32, name="acc", tag="bank%d" % bank)
            cols = slice(t * P, (t + 1) * P)
            nc.tensor.matmul_mx(
                out=acc[:],
                lhsT=wq[0][:, cols].bitcast(FP8X4),
                lhsT_scale=wq[1][:, cols],
                rhs=xq[0][:].bitcast(FP8X4),
                rhs_scale=xq[1][:],
                start=True,
                stop=True,
            )
            own = "%s%d" % (name, t)
            rows = keep.tile([P, S], F32, name=own, tag=tag or own, align_bytes=ALIGN)
            nc.scalar.copy(rows[:], acc[:])
            return rows

        def add_transposed(dst, first, second):
            nc.tensor.matmul(dst, first, ident[:], start=True, stop=False, is_transpose=True)
            nc.tensor.matmul(dst, second, ident[:], start=False, stop=True, is_transpose=True)

        low, high = slice(0, 2), slice(2, 4)
        flat = "p t m j -> p (t m j)"

        x_rows = xT.rearrange("(p j) c -> p j c", j=PACK)
        planes = [keep.tile([P, T], F32, name="plane%d" % j) for j in range(PACK)]
        nc.sync.dma_start(planes[0][:], x_rows[:, 0, :])
        offs_t = load_list(offs, "offs_t")
        for j in range(1, PACK):
            nc.sync.dma_start(planes[j][:], x_rows[:, j, :])
        w1_raw = load_weight(w1, "w1")
        w3_raw = load_weight(w3, "w3")
        cen_t = load_list(cen, "cen_t")
        pos_t = [load_list(pos1, "pos1_t"), load_list(pos2, "pos2_t")]
        w2_raw = load_weight(w2, "w2")
        ident = keep.tile([P, P], F32, name="ident")
        make_identity(nc, ident[:])

        picked = [keep.tile([P, 2, S], BF16, name="picked%d" % u) for u in range(2)]
        x_woven = keep.tile([P, S, PACK], BF16, name="x_woven", align_bytes=ALIGN)
        for j in range(PACK):
            nc.vector.tensor_copy(picked[j // 2][:, j % 2, :], planes[j][:].indirect(offs_t[:]))
        nc.scalar.copy(x_woven[:, :, low], picked[0][:].rearrange("p j c -> p c j"))
        nc.vector.tensor_copy(x_woven[:, :, high], picked[1][:].rearrange("p j c -> p c j"))
        xq = mx_tiles(S, "x")
        quantize(xq, x_woven[:].rearrange("p c j -> p (c j)"), 0, S)

        w1_dealt = dealt_tile("w1_dealt")
        w1q = mx_tiles(N, "w1")
        for u in range(HALVES):
            deal_half(nc.scalar.copy, w1_dealt, w1_raw[u], u)
        for c0, c1 in ((0, P), (P, 2 * P), (2 * P, N)):
            quantize(w1q, w1_dealt[:].rearrange(flat), c0, c1)
        w3_dealt = dealt_tile("w3_dealt")
        deal_half(nc.scalar.copy, w3_dealt, w3_raw[0], 0)
        g = [product(w1q, t, "g", bank=t) for t in range(PACK)]
        deal_half(nc.vector.tensor_copy, w3_dealt, w3_raw[1], 1)
        w3q = mx_tiles(N, "w3")
        quantize(w3q, w3_dealt[:].rearrange(flat), 0, N)

        gain = keep.tile([P, PACK, V], F32, name="gain")
        for t in range(PACK):
            nc.vector.tensor_copy(gain[:, t, :], g[t][:].indirect(cen_t[:]))

        w2_dealt = dealt_tile("w2_dealt")
        h = []
        for u in range(HALVES):
            deal_half(nc.scalar.copy, w2_dealt, w2_raw[u], u)
            h.append(product(w3q, u, "h", bank=4 + u, tag="w2_raw%d" % u))

        scaled = {}

        def scale(t, d, tag=None):
            own = "scaled%d_%d" % (t, d)
            scaled[t, d] = keep.tile([P, V], F32, name=own, tag=tag or own, align_bytes=ALIGN)
            nc.vector.tensor_tensor(scaled[t, d][:], h[t][:].indirect(pos_t[d][:]), gain[:, t, :], MULT)

        w2q = mx_tiles(N, "w2")
        scale(0, 0)
        quantize(w2q, w2_dealt[:].rearrange(flat), 0, N)
        scale(0, 1, tag="w2_dealt")
        h.append(product(w3q, 2, "h", bank=5))
        s = [product(w2q, t, "s", bank=6 + t) for t in range(2)]
        h.append(product(w3q, 3, "h", bank=5))
        s.extend(product(w2q, t, "s", bank=t - 2) for t in range(2, PACK))

        shift = [keep.tile([P, V], F32, name="shift%d" % t) for t in range(PACK)]
        y = [keep.tile([P, 2, V], F32, name="y%d" % u) for u in range(2)]
        out_rows = out_0.rearrange("(p t) v -> p t v", t=PACK)

        def fetch_shift(t):
            nc.vector.tensor_copy(shift[t][:], s[t][:].indirect(cen_t[:]))

        def store(t):
            nc.sync.dma_start(out_rows[:, t, :], y[t // 2][:, t % 2, :])

        def relu_on_tensor(t):
            turned = psum.tile([P, NEIGHBOURS, HALVES, P], F32, name="turned", tag="bank%d" % (2 + t))
            for d in range(NEIGHBOURS):
                for u in range(HALVES):
                    cols = slice(u * P, (u + 1) * P)
                    add_transposed(turned[:, d, u, :], scaled[t, d][:, cols], shift[t][:, cols])
            rect = keep.tile([P, NEIGHBOURS, HALVES, P], F32, name="rect%d" % t)
            nc.scalar.activation(rect[:], turned[:], RELU)
            return rect

        def sum_on_tensor(t, rect):
            back = psum.tile([P, HALVES, P], F32, name="back", tag="bank%d" % (4 + t))
            for u in range(HALVES):
                add_transposed(back[:, u, :], rect[:, 0, u, :], rect[:, 1, u, :])
            nc.scalar.copy(y[t // 2][:, t % 2, :], back[:].rearrange("p u v -> p (u v)"))
            store(t)

        def finish_on_vector(t):
            shifted = keep.tile([P, NEIGHBOURS, V], F32, name="shifted%d" % t)
            for d in range(NEIGHBOURS):
                nc.vector.tensor_tensor(shifted[:, d, :], scaled[t, d][:], shift[t][:], ADD)
            first = keep.tile([P, V], F32, name="first%d" % t)
            nc.vector.tensor_scalar_max(first[:], shifted[:, 0, :], 0.0)
            nc.vector.scalar_tensor_tensor(y[t // 2][:, t % 2, :], shifted[:, 1, :], 0.0, first[:], MAX, ADD)
            store(t)

        for d in range(NEIGHBOURS):
            scale(1, d)
        rects = []
        for t in range(2):
            fetch_shift(t)
            rects.append(relu_on_tensor(t))
        for t in range(2):
            sum_on_tensor(t, rects[t])
        for d in range(NEIGHBOURS):
            scale(2, d, tag="s%d" % d)
        for t in range(2, PACK):
            fetch_shift(t)
        for d in range(NEIGHBOURS):
            scale(3, d, tag="s%d" % (2 + d))
        for t in range(2, PACK):
            finish_on_vector(t)

        y_woven = keep.tile([P, V, PACK], BF16, name="y_woven", align_bytes=ALIGN)
        nc.scalar.copy(y_woven[:, :, low], y[0][:].rearrange("p t c -> p c t"))
        nc.vector.tensor_copy(y_woven[:, :, high], y[1][:].rearrange("p t c -> p c t"))
        yq = mx_tiles(V, "y")
        quantize(yq, y_woven[:].rearrange("p c t -> p (c t)"), 0, V)
        nc.sync.dma_start(out_1[0].rearrange("p c r -> p (c r)").bitcast(I32), yq[0][:].bitcast(I32))
        for q in range(P // 32):
            queue = nc.scalar if q % 2 else nc.sync
            queue.dma_start(out_2[0, 4 * q : 4 * q + 4, :].bitcast(I32), yq[1][32 * q : 32 * q + 4, :].bitcast(I32))
